import numpy as np
import ml_dtypes


def mxq(x, axis, fmt="e4m3"):
    dtype, down = {"e4m3": (ml_dtypes.float8_e4m3fn, 7), "e5m2": (ml_dtypes.float8_e5m2, 14)}[fmt]
    v = np.moveaxis(np.asarray(x, np.float32).astype(ml_dtypes.bfloat16).astype(np.float64), axis, -1)
    blocks = v.reshape(v.shape[:-1] + (-1, 32))
    amax = np.abs(blocks).max(-1, keepdims=True)
    byte = np.maximum(np.where(amax > 0, np.frexp(amax)[1] - 1 + 127, 0) - down, 1)
    scale = np.exp2(byte - 127.0)
    codes = (blocks / scale).astype(np.float32).astype(dtype).astype(np.float64)
    return np.moveaxis((codes * scale).reshape(v.shape), -1, axis)


WIDE = False


def mx_kscale(k):
    if not WIDE:
        return np.ones(k)
    levels = np.array([10, -10, 5, -5, 0])
    if k % 512:
        return np.exp2(np.random.permutation(np.resize(levels, k // 32))).repeat(32)
    a = np.empty((k // 512, 16))
    for p in range(k // 512):
        a[p, :8] = np.random.permutation(np.resize(levels, 8))
        for g in range(8):
            far = levels[np.abs(levels - a[p, g]) >= 10]
            a[p, g + 8] = far[np.random.randint(len(far))]
    return np.exp2(a.ravel()).repeat(32)


def f64(x):
    return np.asarray(x).astype(np.float64)


def striped(idx):
    return np.tile(np.asarray(idx).reshape(-1, 16).T, (8, 1)).astype(np.uint16)


def unstriped(offs):
    return offs[:16].T.reshape(-1).astype(np.int64)


E2M1 = np.array([0.0, 0.5, 1.0, 1.5, 2.0, 3.0, 4.0, 6.0, -0.0, -0.5, -1.0, -1.5, -2.0, -3.0, -4.0, -6.0])


def pack_weight(w, fmt):
    k, n = w.shape
    w = f64(np.asarray(w, np.float32).astype(ml_dtypes.bfloat16)).reshape(k // 32, 32, n)
    amax = np.abs(w).max(1)
    if fmt == "e4m3":
        byte = np.frexp(amax)[1] - 1 + 127 - 7
    else:
        mant, ex = np.frexp(amax / 6.0)
        byte = np.where(mant > 0.5, ex, ex - 1) + 127
    byte = np.clip(np.where(amax > 0, byte, 1), 1, 254)
    scaled = (w * np.exp2(127.0 - byte)[:, None, :]).reshape(k, n).astype(np.float32)
    by_word = np.ascontiguousarray(scaled.reshape(k // 512, 128, 4, n).transpose(0, 1, 3, 2))
    if fmt == "e4m3":
        words = by_word.astype(ml_dtypes.float8_e4m3fn).view(np.uint8)
    else:
        c = by_word.astype(ml_dtypes.float4_e2m1fn).view(np.uint8) & 0xF
        words = (c[..., 0::2] | (c[..., 1::2] << 4)).reshape(k // 512, 128, 2 * n)
    return np.ascontiguousarray(words), np.ascontiguousarray(byte.astype(np.uint8).reshape(k // 512, 16, n))


def unpack_weight(words, scales, fmt):
    g, _, n = scales.shape
    words = np.ascontiguousarray(words).reshape(g, 128, n, -1)
    if fmt == "e4m3":
        vals = words.view(ml_dtypes.float8_e4m3fn).astype(np.float64)
    else:
        nib = np.empty((g, 128, n, 4), np.uint8)
        nib[..., 0::2] = words & 0xF
        nib[..., 1::2] = words >> 4
        vals = E2M1[nib]
    vals = vals * np.repeat(np.exp2(scales.astype(np.float64) - 127.0), 8, axis=1)[..., None]
    return vals.transpose(0, 1, 3, 2).reshape(g * 512, n)


def sigmoid(v):
    return 1.0 / (1.0 + np.exp(-v))


D, E, T, I, Q = 512, 512, 2048, 512, 128


def setup_inputs():
    n = np.random.standard_normal
    idx = np.random.permutation(T)[:I]
    fd = mx_kscale(D)
    fe = mx_kscale(E)
    keysp = pack_weight(n((D, T)) / fd[:, None], "e2m1")
    valsp = pack_weight(n((E, T)) / fe[:, None], "e2m1")
    return {
        "query": (n((D, Q)) * 0.6 / np.sqrt(D) * fd[:, None]).astype(np.float32),
        "keys_words": keysp[0],
        "keys_scales": keysp[1],
        "th": (np.random.uniform(5.8, 6.8, (Q, 1))).astype(np.float32),
        "steep": (np.random.uniform(1.0, 4.0, (Q, 1))).astype(np.float32),
        "kdot": (np.random.uniform(-1.0, 1.0, (Q, 1))).astype(np.float32),
        "gout": (n((E, Q)) * 1 / np.sqrt(E) * fe[:, None]).astype(np.float32),
        "vals_words": valsp[0],
        "vals_scales": valsp[1],
        "dquery": (n((D, Q)) * 1.0 / np.sqrt(D) * fd[:, None]).astype(np.float32),
        "base": (0.5 * n((Q, T))).astype(np.float32),
        "offs": striped(idx),
    }


def reference(query, keys_words, keys_scales, th, steep, kdot, gout, vals_words, vals_scales, dquery, base, offs):
    idx = unstriped(offs)
    keysu = unpack_weight(keys_words, keys_scales, "e2m1")
    valsu = unpack_weight(vals_words, vals_scales, "e2m1")
    queryq = mxq(f64(query), 0, "e4m3")
    keysidxg = keysu[:, idx]
    a = queryq.T @ keysidxg
    dqueryq = mxq(f64(dquery), 0, "e4m3")
    ta = dqueryq.T @ keysidxg
    p = np.exp(a)
    z = np.sum(p, axis=1, keepdims=True)
    gt = sigmoid((np.log(z) - f64(th)) * f64(steep))
    goutq = mxq(f64(gout), 0, "e4m3")
    valsidxg = valsu[:, idx]
    c0 = goutq.T @ valsidxg
    dgt = np.sum(p * c0, axis=1, keepdims=True) / z - f64(kdot)
    dz = dgt * gt * (1.0 - gt) * f64(steep) / z - gt * np.sum(p * c0, axis=1, keepdims=True) / np.square(z)
    dp = gt / z * c0 + dz
    tp = ta * p
    tz = np.sum(tp, axis=1, keepdims=True)
    tgt = tz / z * f64(steep) * gt * (1.0 - gt)
    tdgt = (np.sum(tp * c0, axis=1, keepdims=True) - tz * np.sum(p * c0, axis=1, keepdims=True) / z) / z
    tdz = (((tdgt * gt + tgt * dgt) * (1.0 - gt) + tgt * (-1.0) * dgt * gt) * f64(steep) - tz * dgt * gt * (1.0 - gt) * f64(steep) / z) / z - (tgt * np.sum(p * c0, axis=1, keepdims=True) + np.sum(tp * c0, axis=1, keepdims=True) * gt - tz * z * 2.0 * gt * np.sum(p * c0, axis=1, keepdims=True) / np.square(z)) / np.square(z)
    tdp = (tgt - tz * gt / z) / z * c0 + tdz
    tda = tdp * p + tp * dp
    gs = tda * 512.0
    gf = np.zeros((Q, T))
    gf[:, idx] = gs
    y = f64(base) + gf
    return y

@@ -1,0 +1,195 @@
+from contextlib import ExitStack
+
+import concourse.mybir as mybir
+
+F32 = mybir.dt.float32
+BF16 = mybir.dt.bfloat16
+I32 = mybir.dt.int32
+U32 = mybir.dt.uint32
+U16 = mybir.dt.uint16
+U8 = mybir.dt.uint8
+FP8X4 = mybir.dt.float8_e4m3fn_x4
+FP4X4 = mybir.dt.float4_e2m1fn_x4
+ALU = mybir.AluOpType
+ACT = mybir.ActivationFunctionType
+AX = mybir.AxisListType
+
+P = 128
+PACK = 4
+D, T, SLOTS, Q = 512, 2048, 512, 128
+GAIN = 512.0
+EXP_SPAN = 60.0
+STORE_COLS = (512, 512, 512, 256, 256)
+
+FLOPS = 3 * 2 * D * Q * SLOTS
+
+
+def tile_attend_hvupdategate_s_kernel(
+    tc, query, keys_words, keys_scales, th, steep, kdot, gout, vals_words, vals_scales, dquery, base, offs, out
+):
+    nc = tc.nc
+    with ExitStack() as ctx:
+        held = ctx.enter_context(tc.tile_pool(name="held", bufs=1))
+        psum = ctx.enter_context(tc.psum_pool(name="psum", bufs=1))
+
+        def column(name, width=1):
+            return held.tile([P, width], F32, name=name)
+
+        def load_scales(queue, plane, scales):
+            for r in range(4):
+                queue.dma_start(plane[:].bitcast(I32)[r:P:32, :], scales[0].bitcast(I32)[r:16:4, :])
+
+        def load_rows(name, src, tag):
+            raw = held.tile([P, PACK, Q], F32, name=name, tag=tag, align_bytes=64)
+            nc.sync.dma_start(raw[:], src.rearrange("(p j) w -> p j w", j=PACK))
+            return raw
+
+        def interleave(dst, raw):
+            nc.scalar.activation(
+                dst.rearrange("p (c i) t -> p c t i", i=4), raw[:].rearrange("p t (c i) -> p c t i", i=4), ACT.Copy
+            )
+
+        offsets = held.tile([P, SLOTS // 16], U16, name="offsets")
+        key_words = held.tile([P, T], U16, name="key_words", align_bytes=64)
+        key_plane = held.tile([P, T], U8, name="key_plane", align_bytes=64)
+        val_words = held.tile([P, T], U16, name="val_words", align_bytes=64)
+        val_plane = held.tile([P, T], U8, name="val_plane", align_bytes=64)
+        placed = held.tile([P, T], F32, name="placed", align_bytes=64)
+
+        nc.vector.memset(key_plane[:].bitcast(I32), 0)
+        nc.vector.memset(val_plane[:].bitcast(I32), 0)
+        nc.vector.memset(placed[:].bitcast(I32), 0)
+
+        nc.sync.dma_start(offsets[:], offs)
+        nc.sync.dma_start(key_words[:].bitcast(I32), keys_words[0].bitcast(I32))
+        load_scales(nc.scalar, key_plane, keys_scales)
+        q_raw = load_rows("q_raw", query, "q_then_base")
+        dq_raw = load_rows("dq_raw", dquery, "dq_raw")
+        load_scales(nc.sync, val_plane, vals_scales)
+        go_raw = load_rows("go_raw", gout, "go_raw")
+        nc.sync.dma_start(val_words[:].bitcast(I32), vals_words[0].bitcast(I32))
+
+        th_c, s_c, kd_c = column("th_c"), column("s_c"), column("kd_c")
+        nc.sync.dma_start(th_c[:], th)
+        nc.sync.dma_start(s_c[:], steep)
+        nc.sync.dma_start(kd_c[:], kdot)
+
+        powers = column("powers", 2)
+        nc.gpsimd.memset(powers[:, 1:2], -1.0)
+        nc.gpsimd.tensor_scalar(powers[:, 0:1], s_c[:], -1.0, 0.0, ALU.mult, ALU.add)
+        slope = column("slope", 2)
+        nc.gpsimd.tensor_scalar(slope[:, 0:1], s_c[:], -1.0, 0.0, ALU.mult, ALU.add)
+        nc.gpsimd.tensor_scalar(slope[:, 1:2], s_c[:], -1.0, 1.0, ALU.add, ALU.mult)
+        ks, neg_ks, neg_kd = column("ks"), column("neg_ks"), column("neg_kd")
+        nc.gpsimd.tensor_scalar(ks[:], kd_c[:], s_c[:], 1.0, ALU.mult, ALU.mult)
+        nc.gpsimd.tensor_scalar(neg_ks[:], kd_c[:], s_c[:], -1.0, ALU.mult, ALU.mult)
+        nc.gpsimd.tensor_scalar(neg_kd[:], kd_c[:], -1.0, 0.0, ALU.mult, ALU.add)
+
+        q_bf = held.tile([P, Q, PACK], BF16, name="q_bf", align_bytes=64)
+        dg_bf = held.tile([P, 2 * Q, PACK], BF16, name="dg_bf", align_bytes=64)
+        interleave(q_bf[:], q_raw)
+        interleave(dg_bf[:, 0:Q, :], dq_raw)
+        interleave(dg_bf[:, Q : 2 * Q, :], go_raw)
+
+        base_sb = held.tile([P, T], F32, name="base_sb", tag="q_then_base", align_bytes=64)
+        nc.sync.dma_start(base_sb[:], base)
+
+        k_plane = held.tile([P, SLOTS], U8, name="k_plane", align_bytes=64)
+        k_words = held.tile([P, SLOTS], U16, name="k_words", align_bytes=64)
+        v_plane = held.tile([P, SLOTS], U8, name="v_plane", align_bytes=64)
+        nc.vector.tensor_copy(k_plane[:], key_plane[:].indirect(offsets[:]))
+        nc.vector.tensor_copy(k_words[:], key_words[:].indirect(offsets[:]))
+
+        q_codes = held.tile([P, Q], U32, name="q_codes", tag="q_then_v", align_bytes=64)
+        q_plane = held.tile([P, Q], U8, name="q_plane", align_bytes=64)
+        nc.vector.quantize_mx(q_codes[:].bitcast(FP8X4), q_plane[:], q_bf[:].rearrange("p w j -> p (w j)"))
+
+        a_ps = psum.tile([P, SLOTS], F32, name="a_ps")
+        ta_ps = psum.tile([P, SLOTS], F32, name="ta_ps")
+        c_ps = psum.tile([P, SLOTS], F32, name="c_ps")
+        nc.tensor.matmul_mx(
+            a_ps[:], lhsT=q_codes[:].bitcast(FP8X4), lhsT_scale=q_plane[:],
+            rhs=k_words[:].bitcast(FP4X4), rhs_scale=k_plane[:], start=True, stop=True,
+        )
+        nc.vector.tensor_copy(v_plane[:], val_plane[:].indirect(offsets[:]))
+        neg_max = column("neg_max")
+        nc.vector.tensor_reduce(neg_max[:], a_ps[:], AX.X, ALU.max, negate=True)
+        dg_codes = held.tile([P, 2 * Q], U32, name="dg_codes", align_bytes=64)
+        dg_plane = held.tile([P, 2 * Q], U8, name="dg_plane", align_bytes=64)
+        nc.vector.quantize_mx(dg_codes[:].bitcast(FP8X4), dg_plane[:], dg_bf[:].rearrange("p w j -> p (w j)"))
+        nc.tensor.matmul_mx(
+            ta_ps[:], lhsT=dg_codes[:, 0:Q].bitcast(FP8X4), lhsT_scale=dg_plane[:, 0:Q],
+            rhs=k_words[:].bitcast(FP4X4), rhs_scale=k_plane[:], start=True, stop=True,
+        )
+        v_words = held.tile([P, SLOTS], U16, name="v_words", tag="q_then_v", align_bytes=64)
+        nc.vector.tensor_copy(v_words[:], val_words[:].indirect(offsets[:]))
+        nc.tensor.matmul_mx(
+            c_ps[:], lhsT=dg_codes[:, Q : 2 * Q].bitcast(FP8X4), lhsT_scale=dg_plane[:, Q : 2 * Q],
+            rhs=v_words[:].bitcast(FP4X4), rhs_scale=v_plane[:], start=True, stop=True,
+        )
+
+        p = held.tile([P, SLOTS], F32, name="p", align_bytes=64)
+        xz = column("xz", 2)
+        nc.scalar.activation(p[:], a_ps[:], ACT.Exp, bias=neg_max[:], accum_out=xz[:, 1:2])
+
+        gap = column("gap")
+        parts = column("parts", 2)
+        nc.gpsimd.tensor_scalar(gap[:], neg_max[:], th_c[:], -1.0, ALU.add, ALU.mult)
+        nc.gpsimd.tensor_scalar(parts[:, 0:1], gap[:], EXP_SPAN, -EXP_SPAN, ALU.min, ALU.max)
+        nc.gpsimd.tensor_scalar(parts[:, 1:2], parts[:, 0:1], gap[:], s_c[:], ALU.subtract, ALU.mult)
+        eparts = column("eparts", 2)
+        nc.scalar.activation(eparts[:], parts[:], ACT.Exp)
+        nc.scalar.activation(xz[:, 0:1], xz[:, 1:2], ACT.Copy, scale=eparts[:, 0:1])
+        yr = column("yr", 2)
+        nc.gpsimd.tensor_tensor(yr[:], xz[:], powers[:], ALU.pow)
+        den, g = column("den"), column("g")
+        nc.gpsimd.tensor_scalar(den[:], yr[:, 0:1], eparts[:, 1:2], 1.0, ALU.mult, ALU.add)
+        nc.gpsimd.tensor_tensor(g[:], den[:], powers[:, 1:2], ALU.pow)
+        slope_r = column("slope_r", 2)
+        nc.scalar.activation(slope_r[:], slope[:], ACT.Copy, scale=yr[:, 1:2])
+        rk, nb, k1, gs, h, gain = column("rk"), column("nb"), column("k1"), column("gs"), column("h"), column("gain")
+        nc.scalar.activation(rk[:], g[:], ACT.Identity, scale=slope_r[:, 0:1], bias=slope_r[:, 1:2])
+        nc.scalar.activation(nb[:], g[:], ACT.Identity, scale=ks[:], bias=neg_ks[:])
+        nc.scalar.activation(k1[:], g[:], ACT.Identity, scale=slope[:, 0:1], bias=s_c[:])
+        nc.scalar.activation(gs[:], g[:], ACT.Copy, scale=s_c[:])
+        nc.scalar.activation(h[:], k1[:], ACT.Copy, scale=gs[:])
+        coef = column("coef", 2)
+        nc.scalar.activation(coef[:, 0:1], h[:], ACT.Identity, scale=yr[:, 1:2], bias=rk[:])
+        nc.scalar.activation(coef[:, 1:2], h[:], ACT.Copy, scale=neg_kd[:])
+        neg_r = column("neg_r")
+        nc.gpsimd.tensor_scalar(neg_r[:], yr[:, 1:2], -1.0, 0.0, ALU.mult, ALU.add)
+        nc.gpsimd.tensor_scalar(gain[:], g[:], yr[:, 1:2], GAIN, ALU.mult, ALU.mult)
+
+        tp = held.tile([P, SLOTS], F32, name="tp", align_bytes=64)
+        pc = held.tile([P, SLOTS], F32, name="pc", align_bytes=64)
+        s_tp, s_pc, s_v = column("s_tp"), column("s_pc"), column("s_v")
+        nc.vector.scalar_tensor_tensor(tp[:], ta_ps[:], 1.0, p[:], ALU.mult, ALU.mult, accum_out=s_tp[:])
+        nc.vector.scalar_tensor_tensor(pc[:], c_ps[:], 1.0, p[:], ALU.mult, ALU.mult, accum_out=s_pc[:])
+
+        a1, neg_b, const = column("a1"), column("neg_b"), column("const")
+        coef_b = column("coef_b", 2)
+        nc.scalar.activation(a1[:], s_tp[:], ACT.Copy, scale=rk[:])
+        nc.scalar.activation(neg_b[:], s_tp[:], ACT.Copy, scale=neg_r[:])
+        nc.scalar.activation(coef_b[:], coef[:], ACT.Copy, scale=neg_b[:])
+        nc.scalar.activation(const[:], s_pc[:], ACT.Identity, scale=coef_b[:, 0:1], bias=coef_b[:, 1:2])
+
+        a2, u = column("a2"), column("u")
+        v = held.tile([P, SLOTS], F32, name="v", align_bytes=64)
+        a1pc = held.tile([P, SLOTS], F32, name="a1pc", align_bytes=64)
+        w = held.tile([P, SLOTS], F32, name="w", align_bytes=64)
+        nc.vector.tensor_scalar(a2[:], s_pc[:], rk[:], nb[:], ALU.mult, ALU.add)
+        nc.scalar.activation(a1pc[:], pc[:], ACT.Copy, scale=a1[:])
+        nc.vector.scalar_tensor_tensor(v[:], c_ps[:], a2[:], tp[:], ALU.add, ALU.mult, accum_out=s_v[:])
+        nc.vector.tensor_scalar(u[:], s_v[:], rk[:], const[:], ALU.mult, ALU.add)
+        nc.vector.scalar_tensor_tensor(w[:], p[:], u[:], a1pc[:], ALU.mult, ALU.add)
+        nc.vector.tensor_tensor(placed[:].indirect(offsets[:]), v[:], w[:], ALU.add)
+
+        result = held.tile([P, T], F32, name="result", align_bytes=64)
+        c0 = 0
+        for width in STORE_COLS:
+            cols = slice(c0, c0 + width)
+            nc.vector.scalar_tensor_tensor(
+                result[:, cols], placed[:, cols], gain[:], base_sb[:, cols], ALU.mult, ALU.add
+            )
+            nc.sync.dma_start(out[:, cols], result[:, cols])
+            c0 = c0 + width

@@ -52,7 +52,7 @@ def tile_attend_hvupdategate_s_kernel(
         offsets = held.tile([P, SLOTS // 16], U16, name="offsets")
         key_words = held.tile([P, T], U16, name="key_words", align_bytes=64)
         key_plane = held.tile([P, T], U8, name="key_plane", align_bytes=64)
-        val_words = held.tile([P, T], U16, name="val_words", align_bytes=64)
+        val_words = held.tile([P, T], U16, name="val_words", tag="val_then_tp", align_bytes=64)
         val_plane = held.tile([P, T], U8, name="val_plane", align_bytes=64)
         placed = held.tile([P, T], F32, name="placed", align_bytes=64)
 
@@ -62,31 +62,39 @@ def tile_attend_hvupdategate_s_kernel(
 
         nc.sync.dma_start(offsets[:], offs)
         nc.sync.dma_start(key_words[:].bitcast(I32), keys_words[0].bitcast(I32))
-        load_scales(nc.scalar, key_plane, keys_scales)
+        load_scales(nc.sync, key_plane, keys_scales)
         q_raw = load_rows("q_raw", query, "q_then_base")
-        dq_raw = load_rows("dq_raw", dquery, "dq_raw")
         load_scales(nc.sync, val_plane, vals_scales)
+        dq_raw = load_rows("dq_raw", dquery, "dq_raw")
         go_raw = load_rows("go_raw", gout, "go_raw")
         nc.sync.dma_start(val_words[:].bitcast(I32), vals_words[0].bitcast(I32))
 
         th_c, s_c, kd_c = column("th_c"), column("s_c"), column("kd_c")
-        nc.sync.dma_start(th_c[:], th)
-        nc.sync.dma_start(s_c[:], steep)
-        nc.sync.dma_start(kd_c[:], kdot)
+        nc.scalar.dma_start(th_c[:], th)
+        nc.scalar.dma_start(s_c[:], steep)
+        nc.scalar.dma_start(kd_c[:], kdot)
 
-        powers = column("powers", 2)
-        nc.gpsimd.memset(powers[:, 1:2], -1.0)
-        nc.gpsimd.tensor_scalar(powers[:, 0:1], s_c[:], -1.0, 0.0, ALU.mult, ALU.add)
-        slope = column("slope", 2)
-        nc.gpsimd.tensor_scalar(slope[:, 0:1], s_c[:], -1.0, 0.0, ALU.mult, ALU.add)
-        nc.gpsimd.tensor_scalar(slope[:, 1:2], s_c[:], -1.0, 1.0, ALU.add, ALU.mult)
-        ks, neg_ks, neg_kd = column("ks"), column("neg_ks"), column("neg_kd")
+        consts = column("consts", 4)
+        quarter, ks, neg_ks, neg_half_s, neg_kq = (
+            column("quarter"), column("ks"), column("neg_ks"), column("neg_half_s"), column("neg_kq")
+        )
+        neg_th, upper, lower = column("neg_th"), column("upper"), column("lower")
+        nc.gpsimd.memset(consts[:, 3:4], -1.0)
+        nc.gpsimd.tensor_scalar(neg_th[:], th_c[:], -1.0, 0.0, ALU.mult, ALU.add)
+        nc.gpsimd.tensor_scalar(upper[:], th_c[:], -1.0, EXP_SPAN, ALU.mult, ALU.add)
+        nc.gpsimd.tensor_scalar(lower[:], th_c[:], -1.0, -EXP_SPAN, ALU.mult, ALU.add)
+        nc.gpsimd.tensor_scalar(consts[:, 2:3], s_c[:], -1.0, 0.0, ALU.mult, ALU.add)
+        nc.gpsimd.tensor_scalar(consts[:, 0:1], s_c[:], -1.0, 1.0, ALU.add, ALU.mult)
+        nc.gpsimd.tensor_scalar(quarter[:], s_c[:], s_c[:], 0.25, ALU.mult, ALU.mult)
+        nc.gpsimd.tensor_scalar(neg_half_s[:], s_c[:], -0.5, 0.0, ALU.mult, ALU.add)
+        nc.gpsimd.tensor_scalar(consts[:, 1:2], quarter[:], consts[:, 0:1], 1.0, ALU.add, ALU.mult)
         nc.gpsimd.tensor_scalar(ks[:], kd_c[:], s_c[:], 1.0, ALU.mult, ALU.mult)
         nc.gpsimd.tensor_scalar(neg_ks[:], kd_c[:], s_c[:], -1.0, ALU.mult, ALU.mult)
-        nc.gpsimd.tensor_scalar(neg_kd[:], kd_c[:], -1.0, 0.0, ALU.mult, ALU.add)
+        nc.gpsimd.tensor_scalar(neg_kq[:], kd_c[:], quarter[:], -1.0, ALU.mult, ALU.mult)
+        powers = consts[:, 2:4]
 
-        q_bf = held.tile([P, Q, PACK], BF16, name="q_bf", align_bytes=64)
-        dg_bf = held.tile([P, 2 * Q, PACK], BF16, name="dg_bf", align_bytes=64)
+        q_bf = held.tile([P, Q, PACK], BF16, name="q_bf", tag="q_bf_then_v_plane", align_bytes=64)
+        dg_bf = held.tile([P, 2 * Q, PACK], BF16, name="dg_bf", tag="dg_then_v_words", align_bytes=64)
         interleave(q_bf[:], q_raw)
         interleave(dg_bf[:, 0:Q, :], dq_raw)
         interleave(dg_bf[:, Q : 2 * Q, :], go_raw)
@@ -96,11 +104,10 @@ def tile_attend_hvupdategate_s_kernel(
 
         k_plane = held.tile([P, SLOTS], U8, name="k_plane", align_bytes=64)
         k_words = held.tile([P, SLOTS], U16, name="k_words", align_bytes=64)
-        v_plane = held.tile([P, SLOTS], U8, name="v_plane", align_bytes=64)
         nc.vector.tensor_copy(k_plane[:], key_plane[:].indirect(offsets[:]))
         nc.vector.tensor_copy(k_words[:], key_words[:].indirect(offsets[:]))
 
-        q_codes = held.tile([P, Q], U32, name="q_codes", tag="q_then_v", align_bytes=64)
+        q_codes = held.tile([P, Q], U32, name="q_codes", tag="q_codes_then_v_plane", align_bytes=64)
         q_plane = held.tile([P, Q], U8, name="q_plane", align_bytes=64)
         nc.vector.quantize_mx(q_codes[:].bitcast(FP8X4), q_plane[:], q_bf[:].rearrange("p w j -> p (w j)"))
 
@@ -111,9 +118,13 @@ def tile_attend_hvupdategate_s_kernel(
             a_ps[:], lhsT=q_codes[:].bitcast(FP8X4), lhsT_scale=q_plane[:],
             rhs=k_words[:].bitcast(FP4X4), rhs_scale=k_plane[:], start=True, stop=True,
         )
-        nc.vector.tensor_copy(v_plane[:], val_plane[:].indirect(offsets[:]))
+        half = SLOTS // 2
+        v_lo = held.tile([P, half], U8, name="v_lo", tag="q_bf_then_v_plane", align_bytes=64)
+        nc.vector.tensor_copy(v_lo[:], val_plane[:].indirect(offsets[:, 0 : half // 16]))
         neg_max = column("neg_max")
         nc.vector.tensor_reduce(neg_max[:], a_ps[:], AX.X, ALU.max, negate=True)
+        v_hi = held.tile([P, half], U8, name="v_hi", tag="q_codes_then_v_plane", align_bytes=64)
+        nc.vector.tensor_copy(v_hi[:], val_plane[:].indirect(offsets[:, half // 16 : SLOTS // 16]))
         dg_codes = held.tile([P, 2 * Q], U32, name="dg_codes", align_bytes=64)
         dg_plane = held.tile([P, 2 * Q], U8, name="dg_plane", align_bytes=64)
         nc.vector.quantize_mx(dg_codes[:].bitcast(FP8X4), dg_plane[:], dg_bf[:].rearrange("p w j -> p (w j)"))
@@ -121,57 +132,54 @@ def tile_attend_hvupdategate_s_kernel(
             ta_ps[:], lhsT=dg_codes[:, 0:Q].bitcast(FP8X4), lhsT_scale=dg_plane[:, 0:Q],
             rhs=k_words[:].bitcast(FP4X4), rhs_scale=k_plane[:], start=True, stop=True,
         )
-        v_words = held.tile([P, SLOTS], U16, name="v_words", tag="q_then_v", align_bytes=64)
+        v_words = held.tile([P, SLOTS], U16, name="v_words", tag="dg_then_v_words", align_bytes=64)
         nc.vector.tensor_copy(v_words[:], val_words[:].indirect(offsets[:]))
-        nc.tensor.matmul_mx(
-            c_ps[:], lhsT=dg_codes[:, Q : 2 * Q].bitcast(FP8X4), lhsT_scale=dg_plane[:, Q : 2 * Q],
-            rhs=v_words[:].bitcast(FP4X4), rhs_scale=v_plane[:], start=True, stop=True,
-        )
+        for piece, v_plane in enumerate((v_lo, v_hi)):
+            slots = slice(piece * half, (piece + 1) * half)
+            nc.tensor.matmul_mx(
+                c_ps[:, slots], lhsT=dg_codes[:, Q : 2 * Q].bitcast(FP8X4), lhsT_scale=dg_plane[:, Q : 2 * Q],
+                rhs=v_words[:, slots].bitcast(FP4X4), rhs_scale=v_plane[:], start=True, stop=True,
+            )
 
         p = held.tile([P, SLOTS], F32, name="p", align_bytes=64)
         xz = column("xz", 2)
         nc.scalar.activation(p[:], a_ps[:], ACT.Exp, bias=neg_max[:], accum_out=xz[:, 1:2])
 
-        gap = column("gap")
-        parts = column("parts", 2)
-        nc.gpsimd.tensor_scalar(gap[:], neg_max[:], th_c[:], -1.0, ALU.add, ALU.mult)
-        nc.gpsimd.tensor_scalar(parts[:, 0:1], gap[:], EXP_SPAN, -EXP_SPAN, ALU.min, ALU.max)
-        nc.gpsimd.tensor_scalar(parts[:, 1:2], parts[:, 0:1], gap[:], s_c[:], ALU.subtract, ALU.mult)
-        eparts = column("eparts", 2)
-        nc.scalar.activation(eparts[:], parts[:], ACT.Exp)
-        nc.scalar.activation(xz[:, 0:1], xz[:, 1:2], ACT.Copy, scale=eparts[:, 0:1])
+        near, rest, e_near, e_rest = column("near"), column("rest"), column("e_near"), column("e_rest")
+        nc.gpsimd.tensor_scalar(near[:], neg_max[:], upper[:], lower[:], ALU.min, ALU.max)
+        nc.gpsimd.tensor_scalar(rest[:], near[:], neg_max[:], consts[:, 2:3], ALU.subtract, ALU.mult)
+        nc.scalar.activation(e_near[:], near[:], ACT.Exp, scale=-1.0, bias=neg_th[:])
+        nc.scalar.activation(xz[:, 0:1], xz[:, 1:2], ACT.Copy, scale=e_near[:])
+        nc.scalar.activation(e_rest[:], rest[:], ACT.Exp)
         yr = column("yr", 2)
-        nc.gpsimd.tensor_tensor(yr[:], xz[:], powers[:], ALU.pow)
+        nc.gpsimd.tensor_tensor(yr[:], xz[:], powers, ALU.pow)
         den, g = column("den"), column("g")
-        nc.gpsimd.tensor_scalar(den[:], yr[:, 0:1], eparts[:, 1:2], 1.0, ALU.mult, ALU.add)
-        nc.gpsimd.tensor_tensor(g[:], den[:], powers[:, 1:2], ALU.pow)
-        slope_r = column("slope_r", 2)
-        nc.scalar.activation(slope_r[:], slope[:], ACT.Copy, scale=yr[:, 1:2])
-        rk, nb, k1, gs, h, gain = column("rk"), column("nb"), column("k1"), column("gs"), column("h"), column("gain")
-        nc.scalar.activation(rk[:], g[:], ACT.Identity, scale=slope_r[:, 0:1], bias=slope_r[:, 1:2])
+        nc.gpsimd.tensor_scalar(den[:], yr[:, 0:1], e_rest[:], 1.0, ALU.mult, ALU.add)
+        nc.gpsimd.tensor_tensor(g[:], den[:], consts[:, 3:4], ALU.pow)
+        over_z = column("over_z", 4)
+        nc.scalar.activation(over_z[:], consts[:], ACT.Copy, scale=yr[:, 1:2])
+        neg_r = over_z[:, 3:4]
+        rk, nb, sq, lin, gain = column("rk"), column("nb"), column("sq"), column("lin"), column("gain")
+        nc.scalar.activation(rk[:], g[:], ACT.Identity, scale=over_z[:, 2:3], bias=over_z[:, 0:1])
         nc.scalar.activation(nb[:], g[:], ACT.Identity, scale=ks[:], bias=neg_ks[:])
-        nc.scalar.activation(k1[:], g[:], ACT.Identity, scale=slope[:, 0:1], bias=s_c[:])
-        nc.scalar.activation(gs[:], g[:], ACT.Copy, scale=s_c[:])
-        nc.scalar.activation(h[:], k1[:], ACT.Copy, scale=gs[:])
+        nc.scalar.activation(sq[:], g[:], ACT.Square, scale=s_c[:], bias=neg_half_s[:])
+        nc.scalar.activation(lin[:], g[:], ACT.Identity, scale=over_z[:, 2:3], bias=over_z[:, 1:2])
         coef = column("coef", 2)
-        nc.scalar.activation(coef[:, 0:1], h[:], ACT.Identity, scale=yr[:, 1:2], bias=rk[:])
-        nc.scalar.activation(coef[:, 1:2], h[:], ACT.Copy, scale=neg_kd[:])
-        neg_r = column("neg_r")
-        nc.gpsimd.tensor_scalar(neg_r[:], yr[:, 1:2], -1.0, 0.0, ALU.mult, ALU.add)
-        nc.gpsimd.tensor_scalar(gain[:], g[:], yr[:, 1:2], GAIN, ALU.mult, ALU.mult)
+        nc.scalar.activation(coef[:, 0:1], sq[:], ACT.Identity, scale=neg_r, bias=lin[:])
+        nc.scalar.activation(coef[:, 1:2], sq[:], ACT.Identity, scale=kd_c[:], bias=neg_kq[:])
 
-        tp = held.tile([P, SLOTS], F32, name="tp", align_bytes=64)
+        tp = held.tile([P, SLOTS], F32, name="tp", tag="val_then_tp", align_bytes=64)
         pc = held.tile([P, SLOTS], F32, name="pc", align_bytes=64)
         s_tp, s_pc, s_v = column("s_tp"), column("s_pc"), column("s_v")
         nc.vector.scalar_tensor_tensor(tp[:], ta_ps[:], 1.0, p[:], ALU.mult, ALU.mult, accum_out=s_tp[:])
         nc.vector.scalar_tensor_tensor(pc[:], c_ps[:], 1.0, p[:], ALU.mult, ALU.mult, accum_out=s_pc[:])
 
-        a1, neg_b, const = column("a1"), column("neg_b"), column("const")
+        a1, const = column("a1"), column("const")
         coef_b = column("coef_b", 2)
         nc.scalar.activation(a1[:], s_tp[:], ACT.Copy, scale=rk[:])
-        nc.scalar.activation(neg_b[:], s_tp[:], ACT.Copy, scale=neg_r[:])
-        nc.scalar.activation(coef_b[:], coef[:], ACT.Copy, scale=neg_b[:])
-        nc.scalar.activation(const[:], s_pc[:], ACT.Identity, scale=coef_b[:, 0:1], bias=coef_b[:, 1:2])
+        nc.gpsimd.tensor_scalar(coef_b[:], coef[:], s_tp[:], neg_r, ALU.mult, ALU.mult)
+        nc.gpsimd.tensor_scalar(const[:], s_pc[:], coef_b[:, 0:1], coef_b[:, 1:2], ALU.mult, ALU.add)
+        nc.gpsimd.tensor_scalar(gain[:], g[:], yr[:, 1:2], GAIN, ALU.mult, ALU.mult)
 
         a2, u = column("a2"), column("u")
         v = held.tile([P, SLOTS], F32, name="v", align_bytes=64)

from contextlib import ExitStack

import concourse.mybir as mybir

F32 = mybir.dt.float32
BF16 = mybir.dt.bfloat16
I32 = mybir.dt.int32
U32 = mybir.dt.uint32
U16 = mybir.dt.uint16
U8 = mybir.dt.uint8
FP8X4 = mybir.dt.float8_e4m3fn_x4
FP4X4 = mybir.dt.float4_e2m1fn_x4
ALU = mybir.AluOpType
ACT = mybir.ActivationFunctionType
AX = mybir.AxisListType

P = 128
PACK = 4
D, T, SLOTS, Q = 512, 2048, 512, 128
GAIN = 512.0
EXP_SPAN = 60.0
STORE_COLS = (512, 512, 512, 256, 256)

FLOPS = 3 * 2 * D * Q * SLOTS


def tile_attend_hvupdategate_s_kernel(
    tc, query, keys_words, keys_scales, th, steep, kdot, gout, vals_words, vals_scales, dquery, base, offs, out
):
    nc = tc.nc
    with ExitStack() as ctx:
        held = ctx.enter_context(tc.tile_pool(name="held", bufs=1))
        psum = ctx.enter_context(tc.psum_pool(name="psum", bufs=1))

        def column(name, width=1):
            return held.tile([P, width], F32, name=name)

        def load_scales(queue, plane, scales):
            for r in range(4):
                queue.dma_start(plane[:].bitcast(I32)[r:P:32, :], scales[0].bitcast(I32)[r:16:4, :])

        def load_rows(name, src, tag):
            raw = held.tile([P, PACK, Q], F32, name=name, tag=tag, align_bytes=64)
            nc.sync.dma_start(raw[:], src.rearrange("(p j) w -> p j w", j=PACK))
            return raw

        def interleave(dst, raw):
            nc.scalar.activation(
                dst.rearrange("p (c i) t -> p c t i", i=4), raw[:].rearrange("p t (c i) -> p c t i", i=4), ACT.Copy
            )

        offsets = held.tile([P, SLOTS // 16], U16, name="offsets")
        key_words = held.tile([P, T], U16, name="key_words", align_bytes=64)
        key_plane = held.tile([P, T], U8, name="key_plane", align_bytes=64)
        val_words = held.tile([P, T], U16, name="val_words", tag="val_then_tp", align_bytes=64)
        val_plane = held.tile([P, T], U8, name="val_plane", align_bytes=64)
        placed = held.tile([P, T], F32, name="placed", align_bytes=64)

        nc.vector.memset(key_plane[:].bitcast(I32), 0)
        nc.vector.memset(val_plane[:].bitcast(I32), 0)
        nc.vector.memset(placed[:].bitcast(I32), 0)

        nc.sync.dma_start(offsets[:], offs)
        nc.sync.dma_start(key_words[:].bitcast(I32), keys_words[0].bitcast(I32))
        load_scales(nc.sync, key_plane, keys_scales)
        q_raw = load_rows("q_raw", query, "q_then_base")
        load_scales(nc.sync, val_plane, vals_scales)
        dq_raw = load_rows("dq_raw", dquery, "dq_raw")
        go_raw = load_rows("go_raw", gout, "go_raw")
        nc.sync.dma_start(val_words[:].bitcast(I32), vals_words[0].bitcast(I32))

        th_c, s_c, kd_c = column("th_c"), column("s_c"), column("kd_c")
        nc.scalar.dma_start(th_c[:], th)
        nc.scalar.dma_start(s_c[:], steep)
        nc.scalar.dma_start(kd_c[:], kdot)

        consts = column("consts", 4)
        quarter, ks, neg_ks, neg_half_s, neg_kq = (
            column("quarter"), column("ks"), column("neg_ks"), column("neg_half_s"), column("neg_kq")
        )
        neg_th, upper, lower = column("neg_th"), column("upper"), column("lower")
        nc.gpsimd.memset(consts[:, 3:4], -1.0)
        nc.gpsimd.tensor_scalar(neg_th[:], th_c[:], -1.0, 0.0, ALU.mult, ALU.add)
        nc.gpsimd.tensor_scalar(upper[:], th_c[:], -1.0, EXP_SPAN, ALU.mult, ALU.add)
        nc.gpsimd.tensor_scalar(lower[:], th_c[:], -1.0, -EXP_SPAN, ALU.mult, ALU.add)
        nc.gpsimd.tensor_scalar(consts[:, 2:3], s_c[:], -1.0, 0.0, ALU.mult, ALU.add)
        nc.gpsimd.tensor_scalar(consts[:, 0:1], s_c[:], -1.0, 1.0, ALU.add, ALU.mult)
        nc.gpsimd.tensor_scalar(quarter[:], s_c[:], s_c[:], 0.25, ALU.mult, ALU.mult)
        nc.gpsimd.tensor_scalar(neg_half_s[:], s_c[:], -0.5, 0.0, ALU.mult, ALU.add)
        nc.gpsimd.tensor_scalar(consts[:, 1:2], quarter[:], consts[:, 0:1], 1.0, ALU.add, ALU.mult)
        nc.gpsimd.tensor_scalar(ks[:], kd_c[:], s_c[:], 1.0, ALU.mult, ALU.mult)
        nc.gpsimd.tensor_scalar(neg_ks[:], kd_c[:], s_c[:], -1.0, ALU.mult, ALU.mult)
        nc.gpsimd.tensor_scalar(neg_kq[:], kd_c[:], quarter[:], -1.0, ALU.mult, ALU.mult)
        powers = consts[:, 2:4]

        q_bf = held.tile([P, Q, PACK], BF16, name="q_bf", tag="q_bf_then_v_plane", align_bytes=64)
        dg_bf = held.tile([P, 2 * Q, PACK], BF16, name="dg_bf", tag="dg_then_v_words", align_bytes=64)
        interleave(q_bf[:], q_raw)
        interleave(dg_bf[:, 0:Q, :], dq_raw)
        interleave(dg_bf[:, Q : 2 * Q, :], go_raw)

        base_sb = held.tile([P, T], F32, name="base_sb", tag="q_then_base", align_bytes=64)
        nc.sync.dma_start(base_sb[:], base)

        k_plane = held.tile([P, SLOTS], U8, name="k_plane", align_bytes=64)
        k_words = held.tile([P, SLOTS], U16, name="k_words", align_bytes=64)
        nc.vector.tensor_copy(k_plane[:], key_plane[:].indirect(offsets[:]))
        nc.vector.tensor_copy(k_words[:], key_words[:].indirect(offsets[:]))

        q_codes = held.tile([P, Q], U32, name="q_codes", tag="q_codes_then_v_plane", align_bytes=64)
        q_plane = held.tile([P, Q], U8, name="q_plane", align_bytes=64)
        nc.vector.quantize_mx(q_codes[:].bitcast(FP8X4), q_plane[:], q_bf[:].rearrange("p w j -> p (w j)"))

        a_ps = psum.tile([P, SLOTS], F32, name="a_ps")
        ta_ps = psum.tile([P, SLOTS], F32, name="ta_ps")
        c_ps = psum.tile([P, SLOTS], F32, name="c_ps")
        nc.tensor.matmul_mx(
            a_ps[:], lhsT=q_codes[:].bitcast(FP8X4), lhsT_scale=q_plane[:],
            rhs=k_words[:].bitcast(FP4X4), rhs_scale=k_plane[:], start=True, stop=True,
        )
        half = SLOTS // 2
        v_lo = held.tile([P, half], U8, name="v_lo", tag="q_bf_then_v_plane", align_bytes=64)
        nc.vector.tensor_copy(v_lo[:], val_plane[:].indirect(offsets[:, 0 : half // 16]))
        neg_max = column("neg_max")
        nc.vector.tensor_reduce(neg_max[:], a_ps[:], AX.X, ALU.max, negate=True)
        v_hi = held.tile([P, half], U8, name="v_hi", tag="q_codes_then_v_plane", align_bytes=64)
        nc.vector.tensor_copy(v_hi[:], val_plane[:].indirect(offsets[:, half // 16 : SLOTS // 16]))
        dg_codes = held.tile([P, 2 * Q], U32, name="dg_codes", align_bytes=64)
        dg_plane = held.tile([P, 2 * Q], U8, name="dg_plane", align_bytes=64)
        nc.vector.quantize_mx(dg_codes[:].bitcast(FP8X4), dg_plane[:], dg_bf[:].rearrange("p w j -> p (w j)"))
        nc.tensor.matmul_mx(
            ta_ps[:], lhsT=dg_codes[:, 0:Q].bitcast(FP8X4), lhsT_scale=dg_plane[:, 0:Q],
            rhs=k_words[:].bitcast(FP4X4), rhs_scale=k_plane[:], start=True, stop=True,
        )
        v_words = held.tile([P, SLOTS], U16, name="v_words", tag="dg_then_v_words", align_bytes=64)
        nc.vector.tensor_copy(v_words[:], val_words[:].indirect(offsets[:]))
        for piece, v_plane in enumerate((v_lo, v_hi)):
            slots = slice(piece * half, (piece + 1) * half)
            nc.tensor.matmul_mx(
                c_ps[:, slots], lhsT=dg_codes[:, Q : 2 * Q].bitcast(FP8X4), lhsT_scale=dg_plane[:, Q : 2 * Q],
                rhs=v_words[:, slots].bitcast(FP4X4), rhs_scale=v_plane[:], start=True, stop=True,
            )

        p = held.tile([P, SLOTS], F32, name="p", align_bytes=64)
        xz = column("xz", 2)
        nc.scalar.activation(p[:], a_ps[:], ACT.Exp, bias=neg_max[:], accum_out=xz[:, 1:2])

        near, rest, e_near, e_rest = column("near"), column("rest"), column("e_near"), column("e_rest")
        nc.gpsimd.tensor_scalar(near[:], neg_max[:], upper[:], lower[:], ALU.min, ALU.max)
        nc.gpsimd.tensor_scalar(rest[:], near[:], neg_max[:], consts[:, 2:3], ALU.subtract, ALU.mult)
        nc.scalar.activation(e_near[:], near[:], ACT.Exp, scale=-1.0, bias=neg_th[:])
        nc.scalar.activation(xz[:, 0:1], xz[:, 1:2], ACT.Copy, scale=e_near[:])
        nc.scalar.activation(e_rest[:], rest[:], ACT.Exp)
        yr = column("yr", 2)
        nc.gpsimd.tensor_tensor(yr[:], xz[:], powers, ALU.pow)
        den, g = column("den"), column("g")
        nc.gpsimd.tensor_scalar(den[:], yr[:, 0:1], e_rest[:], 1.0, ALU.mult, ALU.add)
        nc.gpsimd.tensor_tensor(g[:], den[:], consts[:, 3:4], ALU.pow)
        over_z = column("over_z", 4)
        nc.scalar.activation(over_z[:], consts[:], ACT.Copy, scale=yr[:, 1:2])
        neg_r = over_z[:, 3:4]
        rk, nb, sq, lin, gain = column("rk"), column("nb"), column("sq"), column("lin"), column("gain")
        nc.scalar.activation(rk[:], g[:], ACT.Identity, scale=over_z[:, 2:3], bias=over_z[:, 0:1])
        nc.scalar.activation(nb[:], g[:], ACT.Identity, scale=ks[:], bias=neg_ks[:])
        nc.scalar.activation(sq[:], g[:], ACT.Square, scale=s_c[:], bias=neg_half_s[:])
        nc.scalar.activation(lin[:], g[:], ACT.Identity, scale=over_z[:, 2:3], bias=over_z[:, 1:2])
        coef = column("coef", 2)
        nc.scalar.activation(coef[:, 0:1], sq[:], ACT.Identity, scale=neg_r, bias=lin[:])
        nc.scalar.activation(coef[:, 1:2], sq[:], ACT.Identity, scale=kd_c[:], bias=neg_kq[:])

        tp = held.tile([P, SLOTS], F32, name="tp", tag="val_then_tp", align_bytes=64)
        pc = held.tile([P, SLOTS], F32, name="pc", align_bytes=64)
        s_tp, s_pc, s_v = column("s_tp"), column("s_pc"), column("s_v")
        nc.vector.scalar_tensor_tensor(tp[:], ta_ps[:], 1.0, p[:], ALU.mult, ALU.mult, accum_out=s_tp[:])
        nc.vector.scalar_tensor_tensor(pc[:], c_ps[:], 1.0, p[:], ALU.mult, ALU.mult, accum_out=s_pc[:])

        a1, const = column("a1"), column("const")
        coef_b = column("coef_b", 2)
        nc.scalar.activation(a1[:], s_tp[:], ACT.Copy, scale=rk[:])
        nc.gpsimd.tensor_scalar(coef_b[:], coef[:], s_tp[:], neg_r, ALU.mult, ALU.mult)
        nc.gpsimd.tensor_scalar(const[:], s_pc[:], coef_b[:, 0:1], coef_b[:, 1:2], ALU.mult, ALU.add)
        nc.gpsimd.tensor_scalar(gain[:], g[:], yr[:, 1:2], GAIN, ALU.mult, ALU.mult)

        a2, u = column("a2"), column("u")
        v = held.tile([P, SLOTS], F32, name="v", align_bytes=64)
        a1pc = held.tile([P, SLOTS], F32, name="a1pc", align_bytes=64)
        w = held.tile([P, SLOTS], F32, name="w", align_bytes=64)
        nc.vector.tensor_scalar(a2[:], s_pc[:], rk[:], nb[:], ALU.mult, ALU.add)
        nc.scalar.activation(a1pc[:], pc[:], ACT.Copy, scale=a1[:])
        nc.vector.scalar_tensor_tensor(v[:], c_ps[:], a2[:], tp[:], ALU.add, ALU.mult, accum_out=s_v[:])
        nc.vector.tensor_scalar(u[:], s_v[:], rk[:], const[:], ALU.mult, ALU.add)
        nc.vector.scalar_tensor_tensor(w[:], p[:], u[:], a1pc[:], ALU.mult, ALU.add)
        nc.vector.tensor_tensor(placed[:].indirect(offsets[:]), v[:], w[:], ALU.add)

        result = held.tile([P, T], F32, name="result", align_bytes=64)
        c0 = 0
        for width in STORE_COLS:
            cols = slice(c0, c0 + width)
            nc.vector.scalar_tensor_tensor(
                result[:, cols], placed[:, cols], gain[:], base_sb[:, cols], ALU.mult, ALU.add
            )
            nc.sync.dma_start(out[:, cols], result[:, cols])
            c0 = c0 + width
